import numpy as np
import ml_dtypes


def mxq(x, axis, fmt="e4m3"):
    dtype, down = {"e4m3": (ml_dtypes.float8_e4m3fn, 7), "e5m2": (ml_dtypes.float8_e5m2, 14)}[fmt]
    v = np.moveaxis(np.asarray(x, np.float32).astype(ml_dtypes.bfloat16).astype(np.float64), axis, -1)
    blocks = v.reshape(v.shape[:-1] + (-1, 32))
    amax = np.abs(blocks).max(-1, keepdims=True)
    byte = np.maximum(np.where(amax > 0, np.frexp(amax)[1] - 1 + 127, 0) - down, 1)
    scale = np.exp2(byte - 127.0)
    codes = (blocks / scale).astype(np.float32).astype(dtype).astype(np.float64)
    return np.moveaxis((codes * scale).reshape(v.shape), -1, axis)


WIDE = False


def mx_kscale(k):
    if not WIDE:
        return np.ones(k)
    levels = np.array([10, -10, 5, -5, 0])
    if k % 512:
        return np.exp2(np.random.permutation(np.resize(levels, k // 32))).repeat(32)
    a = np.empty((k // 512, 16))
    for p in range(k // 512):
        a[p, :8] = np.random.permutation(np.resize(levels, 8))
        for g in range(8):
            far = levels[np.abs(levels - a[p, g]) >= 10]
            a[p, g + 8] = far[np.random.randint(len(far))]
    return np.exp2(a.ravel()).repeat(32)


def f64(x):
    return np.asarray(x).astype(np.float64)


def striped(idx):
    return np.tile(idx.reshape(-1, 16).T, (8, 1)).astype(np.uint16)


def unstriped(offs):
    return offs[:16].T.reshape(-1).astype(np.int64)


def pack_weight(w):
    k, n = w.shape
    w = f64(np.asarray(w, np.float32).astype(ml_dtypes.bfloat16)).reshape(k // 32, 32, n)
    amax = np.abs(w).max(1)
    byte = np.clip(np.where(amax > 0, np.frexp(amax)[1] - 1 + 127 - 7, 1), 1, 254)
    scaled = (w * np.exp2(127.0 - byte)[:, None, :]).reshape(k, n).astype(np.float32)
    words = np.ascontiguousarray(scaled.reshape(k // 512, 128, 4, n).transpose(0, 1, 3, 2)).astype(ml_dtypes.float8_e4m3fn).view(np.uint8)
    return words, np.ascontiguousarray(byte.astype(np.uint8).reshape(k // 512, 16, n))


def unpack_weight(words, scales):
    g, p, n, _ = words.shape
    vals = np.ascontiguousarray(words).view(ml_dtypes.float8_e4m3fn).astype(np.float64) * np.repeat(np.exp2(scales.astype(np.float64) - 127.0), 8, axis=1)[..., None]
    return vals.transpose(0, 1, 3, 2).reshape(g * 512, n)


def relu(v):
    return np.maximum(v, 0.0)


K, T, S, D, N, H = 1024, 2048, 1024, 4, 128, 512


def setup_inputs():
    n = np.random.standard_normal
    s = mx_kscale(K)[:, None]
    u = mx_kscale(H)
    packed_xT = pack_weight(n((K, T)) * s)
    return {
        "x_words": packed_xT[0],
        "x_scales": packed_xT[1],
        "w1": (n((K, H)) / np.sqrt(K) / s).astype(np.float32),
        "w2": (n((K, H)) / np.sqrt(K) / s).astype(np.float32),
        "ctf": (np.random.uniform(-1.0, 1.0, (H, S))).astype(np.float32),
        "unit": (np.random.uniform(0.6, 1.4, (H, 1)) * u[:, None]).astype(np.float32),
        "w3": (n((H, N)) / np.sqrt(H) / u[:, None]).astype(np.float32),
        "offs": striped(np.random.permutation(T)[:S]),
        "half": striped(np.random.permutation(S)),
    }


def reference(x_words, x_scales, w1, w2, ctf, unit, w3, offs, half):
    xq = unpack_weight(x_words, x_scales)[:, unstriped(offs)]
    re = mxq(f64(w1), 0, "e4m3").T @ xq
    ra = f64(ctf) * re
    ah = re[:, unstriped(half)]
    rb = f64(ctf) * ah
    xc = ra * rb
    num = xc.reshape(len(xc), -1, D).sum(axis=2)
    pa = (ra) ** 2
    ea = pa.reshape(len(pa), -1, D).sum(axis=2) + 0.3
    pb = (rb) ** 2
    eb = pb.reshape(len(pb), -1, D).sum(axis=2) + 0.3
    fsc = num / np.sqrt(ea * eb)
    wien = relu(fsc + 0.6) / (np.abs(fsc) + 0.5)
    im2 = mxq(f64(w2), 0, "e4m3").T @ xq
    filt = np.repeat(wien, D, axis=1) * ra - (0.4 * im2)
    hid = f64(unit) * filt
    return mxq(f64(w3), 0, "e4m3").T @ mxq(hid, 0, "e4m3")

@@ -1,0 +1,352 @@
+from contextlib import ExitStack
+
+import concourse.mybir as mybir
+from concourse.masks import make_identity
+
+K, T, S, D, N, H = 1024, 2048, 1024, 4, 128, 512
+FLOPS = 2 * (2 * K * H * S + H * N * S)
+
+F32 = mybir.dt.float32
+BF16 = mybir.dt.bfloat16
+I32 = mybir.dt.int32
+U32 = mybir.dt.uint32
+U16 = mybir.dt.uint16
+U8 = mybir.dt.uint8
+FP8X4 = mybir.dt.float8_e4m3fn_x4
+ACT = mybir.ActivationFunctionType
+MULT = mybir.AluOpType.mult
+ADD = mybir.AluOpType.add
+MAX = mybir.AluOpType.max
+
+P = 128
+PACK = 4
+PASSES = K // (P * PACK)
+HALF = S // 2
+CH = S // 4
+NCH = S // CH
+V = CH // D
+
+
+def tile_picked_ycryoem_filt_p_kernel(
+    tc, x_words, x_scales, w1, w2, ctf, unit, w3, offs, half, out
+):
+    nc = tc.nc
+    with ExitStack() as ctx:
+        keep = ctx.enter_context(tc.tile_pool(name="keep", bufs=1))
+        ring = ctx.enter_context(tc.tile_pool(name="ring", bufs=2))
+        psum = ctx.enter_context(tc.psum_pool(name="psum", bufs=1))
+
+        def bank(b, name):
+            return psum.tile([P, 512], F32, name=name, tag="bank%d" % b)
+
+        offs_sb = keep.tile([P, S // 16], U16, name="offs_sb")
+        half_sb = keep.tile([P, S // 16], U16, name="half_sb")
+        xs_tab = keep.tile([P, T], U8, name="xs_tab", align_bytes=64)
+        nc.vector.memset(xs_tab[:].bitcast(I32), 0)
+        nc.sync.dma_start(offs_sb[:], offs)
+
+        def rows(w, g):
+            return w[g * 512 : (g + 1) * 512, :].rearrange("(p j) c -> p j c", j=PACK)
+
+        w1a_raw = keep.tile([P, PACK, H], F32, name="w1a_raw", tag="wraw")
+        nc.sync.dma_start(w1a_raw[:], rows(w1, 0))
+        xs_rows = keep.tile([P, T // 4], I32, name="xs_rows")
+        for q in range(4):
+            live = slice(32 * q, 32 * q + 4 * PASSES)
+            nc.sync.dma_start(xs_rows[live, :], x_scales[:, 4 * q : 4 * q + 4, :].bitcast(I32))
+            nc.vector.tensor_copy(xs_tab[live, :].bitcast(I32), xs_rows[live, :])
+        xw_tab = []
+        for g in range(PASSES):
+            tab = keep.tile([P, T], I32, name="xw_tab%d" % g, align_bytes=64)
+            nc.sync.dma_start(tab[:], x_words[g].rearrange("p n t -> p (n t)").bitcast(I32))
+            xw_tab.append(tab)
+        w1b_raw = []
+        for a in range(2):
+            raw = keep.tile([P, PACK, H // 2], F32, name="w1b_raw%d" % a)
+            nc.sync.dma_start(raw[:], rows(w1, 1)[:, :, a * (H // 2) : (a + 1) * (H // 2)])
+            w1b_raw.append(raw)
+        nc.sync.dma_start(half_sb[:], half)
+        ctf_sb = []
+        for t in range(PACK):
+            c = keep.tile([P, S], F32, name="ctf%d" % t)
+            nc.sync.dma_start(c[:], ctf.rearrange("(p t) j -> p t j", t=PACK)[:, t, :])
+            ctf_sb.append(c)
+        ident = keep.tile([P, P], F32, name="ident")
+        make_identity(nc, ident[:])
+
+        def deal(copy, dst, raw, m0, m1):
+            copy(
+                dst[:, :, m0:m1, :].rearrange("p t m j -> p m j t"),
+                raw[:].rearrange("p j (m t) -> p m j t", t=PACK),
+            )
+
+        def w_tiles(name):
+            codes = keep.tile([P, H], U32, name=name + "_codes", align_bytes=64)
+            scales = keep.tile([P, H], U8, name=name + "_scales", align_bytes=64)
+            return codes, scales
+
+        def quantise(wq, dealt, t0, t1):
+            nc.vector.quantize_mx(
+                out=wq[0][:, t0 * P : t1 * P].bitcast(FP8X4),
+                scales=wq[1][:, t0 * P : t1 * P],
+                in_=dealt[:, t0:t1].rearrange("p t m j -> p (t m j)"),
+            )
+
+        xs = keep.tile([P, S], U8, name="xs", align_bytes=64)
+        nc.vector.tensor_copy(xs[:], xs_tab[:].indirect(offs_sb[:]))
+        w1q = [w_tiles("w1a"), w_tiles("w1b")]
+        dealt = ring.tile([P, PACK, P, PACK], BF16, name="dealt", tag="dealt", align_bytes=64)
+        deal(nc.scalar.copy, dealt, w1a_raw, 0, P)
+        quantise(w1q[0], dealt, 0, PACK)
+        w2a_raw = keep.tile([P, PACK, H], F32, name="w2a_raw", tag="wraw")
+        nc.sync.dma_start(w2a_raw[:], rows(w2, 0))
+        w2b_raw = keep.tile([P, PACK, H], F32, name="w2b_raw")
+        nc.sync.dma_start(w2b_raw[:], rows(w2, 1))
+        unit_sb = keep.tile([P, PACK], F32, name="unit_sb")
+        nc.sync.dma_start(unit_sb[:], unit.rearrange("(p t) o -> p (t o)", t=PACK))
+        w3_raw = keep.tile([P, PACK, N], F32, name="w3_raw")
+        nc.sync.dma_start(w3_raw[:], rows(w3, 0))
+
+        xw = {}
+        for g in range(PASSES):
+            for h in range(2):
+                xw[g, h] = keep.tile([P, HALF], U32, name="xw%d%d" % (g, h), align_bytes=64)
+                nc.vector.tensor_copy(
+                    xw[g, h][:], xw_tab[g][:].bitcast(U32).indirect(offs_sb[:, h * 32 : (h + 1) * 32])
+                )
+
+        def mx_pass(acc, wq, g, t, h):
+            nc.tensor.matmul_mx(
+                out=acc[:],
+                lhsT=wq[g][0][:, t * P : (t + 1) * P].bitcast(FP8X4),
+                lhsT_scale=wq[g][1][:, t * P : (t + 1) * P],
+                rhs=xw[g, h][:].bitcast(FP8X4),
+                rhs_scale=xs[4 * g : P, h * HALF : (h + 1) * HALF],
+                start=(g == 0),
+                stop=(g == PASSES - 1),
+            )
+
+        re_ps = {}
+        for h in range(2):
+            for t in range(PACK):
+                re_ps[t, h] = bank(4 * h + t, "re_ps")
+                mx_pass(re_ps[t, h], w1q, 0, t, h)
+
+        dealt = ring.tile([P, PACK, P, PACK], BF16, name="dealt", tag="dealt", align_bytes=64)
+        deal(nc.scalar.copy, dealt, w1b_raw[0], 0, P // 2)
+        deal(nc.vector.tensor_copy, dealt, w1b_raw[1], P // 2, P)
+
+        re = [keep.tile([P, S], F32, name="re%d" % t) for t in range(PACK)]
+        ra = [keep.tile([P, 2, PACK, CH], F32, name="ra%d" % h) for h in range(2)]
+        gim = [keep.tile([P, 2, PACK, CH], F32, name="gim%d" % h) for h in range(2)]
+
+        def make_ra(t, h):
+            nc.vector.tensor_tensor(
+                ra[h][:, :, t, :],
+                re_ps[t, h][:].rearrange("p (q c) -> p q c", q=2),
+                ctf_sb[t][:, h * HALF : (h + 1) * HALF].rearrange("p (q c) -> p q c", q=2),
+                MULT,
+            )
+
+        rb = {}
+
+        def make_rb(q, t):
+            if t == 0:
+                rb[q] = ring.tile([P, PACK, CH], F32, name="rb", tag="rb")
+            nc.vector.tensor_tensor(
+                rb[q][:, t, :],
+                re[t][:].indirect(half_sb[:, q * (CH // 16) : (q + 1) * (CH // 16)]),
+                ctf_sb[t][:, q * CH : (q + 1) * CH],
+                MULT,
+            )
+
+        for t in range(PACK):
+            quantise(w1q[1], dealt, t, t + 1)
+        for t in range(PACK):
+            for h in range(2):
+                mx_pass(re_ps[t, h], w1q, 1, t, h)
+                nc.scalar.copy(re[t][:, h * HALF : (h + 1) * HALF], re_ps[t, h][:])
+            make_ra(t, 0)
+            make_rb(0, t)
+
+        def ra_chunk(q):
+            return ra[q // 2][:, q % 2]
+
+        def pairs_in(x):
+            return x.rearrange("p t (v a b) -> p (t v) a b", a=2, b=2)
+
+        def pairs_out(x):
+            return x[:].rearrange("p a w b -> p w a b")
+
+        def shell_sum(dst, src):
+            for u in range(2):
+                for a in range(2):
+                    for b in range(2):
+                        nc.tensor.matmul(
+                            dst[:, u * P : (u + 1) * P],
+                            src[:, a, u * P : (u + 1) * P, b],
+                            ident[:],
+                            start=(a == 0 and b == 0),
+                            stop=(a == 1 and b == 1),
+                            is_transpose=True,
+                        )
+
+        e_ps = {}
+        n_ps = {}
+
+        def power_a(q):
+            pa = ring.tile([P, 2, PACK * V, 2], F32, name="pa", tag="pa")
+            nc.scalar.activation(pairs_out(pa), pairs_in(ra_chunk(q)), ACT.Square)
+            e_ps[q] = bank(2 * (q % 2), "e_ps")
+            shell_sum(e_ps[q][:, 0:CH], pa)
+
+        def power_b(q):
+            pb = ring.tile([P, 2, PACK * V, 2], F32, name="pb", tag="pb")
+            nc.scalar.activation(pairs_out(pb), pairs_in(rb[q][:]), ACT.Square)
+            shell_sum(e_ps[q][:, CH : 2 * CH], pb)
+
+        def cross(q):
+            xc = ring.tile([P, 2, PACK * V, 2], F32, name="xc", tag="xc")
+            nc.vector.tensor_tensor(pairs_out(xc), pairs_in(ra_chunk(q)), pairs_in(rb[q][:]), MULT)
+            n_ps[q] = bank(2 * (q % 2) + 1, "n_ps")
+            shell_sum(n_ps[q][:, 0:CH], xc)
+
+        small = {}
+
+        def weight_1(q):
+            rs = ring.tile([P, 2 * CH], F32, name="rs", tag="rs")
+            nc.scalar.activation(rs[:], e_ps[q][:], ACT.Abs_reciprocal_sqrt, bias=0.3)
+            f1 = ring.tile([P, CH], F32, name="f1", tag="f1")
+            nc.vector.tensor_tensor(f1[:], n_ps[q][:, 0:CH], rs[:, 0:CH], MULT)
+            fsc = ring.tile([P, CH], F32, name="fsc", tag="fsc")
+            nc.vector.tensor_tensor(fsc[:], f1[:], rs[:, CH : 2 * CH], MULT)
+            mag = ring.tile([P, CH], F32, name="mag", tag="mag")
+            nc.scalar.activation(mag[:], fsc[:], ACT.Abs)
+            z = ring.tile([P, CH], F32, name="z", tag="z")
+            nc.scalar.activation(z[:], mag[:], ACT.Abs_reciprocal_sqrt, bias=0.5)
+            small[q] = (fsc, z)
+
+        def weight_2(q):
+            fsc, z = small[q]
+            top = ring.tile([P, CH], F32, name="top", tag="top")
+            nc.vector.scalar_tensor_tensor(top[:], fsc[:], 0.6, z[:], ADD, MULT)
+            wien = ring.tile([P, CH], F32, name="wien", tag="wien")
+            nc.vector.scalar_tensor_tensor(wien[:], top[:], 0.0, z[:], MAX, MULT)
+            for u in range(2):
+                nc.tensor.transpose(n_ps[q][:, CH + u * P : CH + (u + 1) * P], wien[:, u * P : (u + 1) * P], ident[:])
+
+        w2q = [w_tiles("w2a"), w_tiles("w2b")]
+
+        def prep_w2(g, raw):
+            d2 = ring.tile([P, PACK, P, PACK], BF16, name="dealt", tag="dealt", align_bytes=64)
+            deal(nc.scalar.copy, d2, raw, 0, P)
+            quantise(w2q[g], d2, 0, PACK)
+
+        neg_unit = keep.tile([P, PACK], F32, name="neg_unit")
+
+        def second_product(h):
+            for t in range(PACK):
+                acc = bank(4 + t, "im_ps")
+                for g in range(PASSES):
+                    mx_pass(acc, w2q, g, t, h)
+                nc.scalar.activation(
+                    gim[h][:, :, t, :],
+                    acc[:].rearrange("p (q c) -> p q c", q=2),
+                    ACT.Copy,
+                    scale=neg_unit[:, t : t + 1],
+                )
+
+        w3_codes = keep.tile([P, N], U32, name="w3_codes", align_bytes=64)
+        w3_scales = keep.tile([P, N], U8, name="w3_scales", align_bytes=64)
+
+        def prep_w3():
+            nc.vector.tensor_scalar(neg_unit[:], unit_sb[:], -0.4, None, MULT)
+            d3 = keep.tile([P, N, PACK], BF16, name="w3_dealt", align_bytes=64)
+            nc.scalar.copy(d3[:], w3_raw[:].rearrange("p j m -> p m j"))
+            nc.vector.quantize_mx(
+                out=w3_codes[:].bitcast(FP8X4), scales=w3_scales[:], in_=d3[:].rearrange("p m j -> p (m j)")
+            )
+
+        hid = {}
+
+        def make_hid(q):
+            fil = ring.tile([P, PACK, CH], F32, name="fil", tag="fil")
+            for t in range(PACK):
+                nc.vector.scalar_tensor_tensor(
+                    fil[:, t, :].rearrange("p (v d) -> p v d", d=D),
+                    n_ps[q][:, CH + t * V : CH + (t + 1) * V].unsqueeze(2).to_broadcast([P, V, D]),
+                    unit_sb[:, t : t + 1],
+                    ra_chunk(q)[:, t, :].rearrange("p (v d) -> p v d", d=D),
+                    MULT,
+                    MULT,
+                )
+            hid[q] = ring.tile([P, CH, PACK], BF16, name="hid", tag="hid", align_bytes=64)
+            nc.vector.tensor_tensor(
+                hid[q][:].rearrange("p (c i) t -> p c t i", i=4),
+                fil[:].rearrange("p t (c i) -> p c t i", i=4),
+                gim[q // 2][:, q % 2].rearrange("p t (c i) -> p c t i", i=4),
+                ADD,
+            )
+
+        def finish(q):
+            codes = ring.tile([P, CH], U32, name="hid_codes", tag="hid_codes", align_bytes=64)
+            scales = ring.tile([P, CH], U8, name="hid_scales", tag="hid_scales", align_bytes=64)
+            nc.vector.quantize_mx(
+                out=codes[:].bitcast(FP8X4), scales=scales[:], in_=hid[q][:].rearrange("p c t -> p (c t)")
+            )
+            acc = bank(4 + q, "out_ps")
+            nc.tensor.matmul_mx(
+                out=acc[:, 0:CH],
+                lhsT=w3_codes[:].bitcast(FP8X4),
+                lhsT_scale=w3_scales[:],
+                rhs=codes[:].bitcast(FP8X4),
+                rhs_scale=scales[:],
+                start=True,
+                stop=True,
+            )
+            res = ring.tile([P, CH], F32, name="res", tag="res")
+            nc.scalar.copy(res[:], acc[:, 0:CH])
+            nc.sync.dma_start(out[:, q * CH : (q + 1) * CH], res[:])
+
+        def gathers(q):
+            for t in range(PACK):
+                make_rb(q, t)
+
+        power_a(0)
+        power_b(0)
+        cross(0)
+        gathers(1)
+        power_a(1)
+        power_b(1)
+        cross(1)
+        for t in range(PACK):
+            make_ra(t, 1)
+        weight_1(0)
+        prep_w2(0, w2a_raw)
+        prep_w2(1, w2b_raw)
+        prep_w3()
+        gathers(2)
+        weight_2(0)
+        second_product(0)
+        weight_1(1)
+        power_a(2)
+        power_b(2)
+        weight_2(1)
+        make_hid(0)
+        cross(2)
+        gathers(3)
+        second_product(1)
+        finish(0)
+        weight_1(2)
+        power_a(3)
+        power_b(3)
+        make_hid(1)
+        cross(3)
+        weight_2(2)
+        finish(1)
+        weight_1(3)
+        make_hid(2)
+        weight_2(3)
+        finish(2)
+        make_hid(3)
+        finish(3)

@@ -25,6 +25,11 @@ HALF = S // 2
 CH = S // 4
 NCH = S // CH
 V = CH // D
+SCALAR_FETCHES = ((3, 0), (1, 1), (3, 1))
+IM_BANKS = ((1, 3, 1, 3), (1, 3, 1, 3))
+HID_PIECES = ((0, 0, 256), (0, 256, 512), (1, 0, 256), (1, 256, 384), (1, 384, 512))
+OUT_BANKS = (0, 2, 4, 6, 0)
+W1B_PIECES = ((0, 64), (64, 96), (96, 128))
 
 
 def tile_picked_ycryoem_filt_p_kernel(
@@ -48,36 +53,41 @@ def tile_picked_ycryoem_filt_p_kernel(
         def rows(w, g):
             return w[g * 512 : (g + 1) * 512, :].rearrange("(p j) c -> p j c", j=PACK)
 
-        w1a_raw = keep.tile([P, PACK, H], F32, name="w1a_raw", tag="wraw")
-        nc.sync.dma_start(w1a_raw[:], rows(w1, 0))
         xs_rows = keep.tile([P, T // 4], I32, name="xs_rows")
         for q in range(4):
             live = slice(32 * q, 32 * q + 4 * PASSES)
             nc.sync.dma_start(xs_rows[live, :], x_scales[:, 4 * q : 4 * q + 4, :].bitcast(I32))
             nc.vector.tensor_copy(xs_tab[live, :].bitcast(I32), xs_rows[live, :])
-        xw_tab = []
-        for g in range(PASSES):
-            tab = keep.tile([P, T], I32, name="xw_tab%d" % g, align_bytes=64)
-            nc.sync.dma_start(tab[:], x_words[g].rearrange("p n t -> p (n t)").bitcast(I32))
-            xw_tab.append(tab)
-        w1b_raw = []
-        for a in range(2):
-            raw = keep.tile([P, PACK, H // 2], F32, name="w1b_raw%d" % a)
-            nc.sync.dma_start(raw[:], rows(w1, 1)[:, :, a * (H // 2) : (a + 1) * (H // 2)])
-            w1b_raw.append(raw)
+        w1a_raw = keep.tile([P, PACK, H], F32, name="w1a_raw", tag="wraw")
+        for c0 in (0, H // 2):
+            nc.sync.dma_start(w1a_raw[:, :, c0 : c0 + H // 2], rows(w1, 0)[:, :, c0 : c0 + H // 2])
+        xw_tab = [keep.tile([P, T], I32, name="xw_tab%d" % g, align_bytes=64) for g in range(PASSES)]
+        w1b_raw = [keep.tile([P, PACK, PACK * (m1 - m0)], F32, name="w1b_raw%d" % m0) for m0, m1 in W1B_PIECES]
+
+        def load_words(g):
+            nc.sync.dma_start(xw_tab[g][:], x_words[g].rearrange("p n t -> p (n t)").bitcast(I32))
+
+        def load_w1b(n):
+            m0, m1 = W1B_PIECES[n]
+            nc.sync.dma_start(w1b_raw[n][:], rows(w1, 1)[:, :, PACK * m0 : PACK * m1])
+
+        load_words(0)
+        load_w1b(0)
+        load_words(1)
+        load_w1b(1)
+        load_w1b(2)
         nc.sync.dma_start(half_sb[:], half)
-        ctf_sb = []
+        ctf_all = keep.tile([P, PACK, S], F32, name="ctf_all")
+        ctf_sb = [ctf_all[:, t, :] for t in range(PACK)]
         for t in range(PACK):
-            c = keep.tile([P, S], F32, name="ctf%d" % t)
-            nc.sync.dma_start(c[:], ctf.rearrange("(p t) j -> p t j", t=PACK)[:, t, :])
-            ctf_sb.append(c)
+            nc.sync.dma_start(ctf_sb[t], ctf.rearrange("(p t) j -> p t j", t=PACK)[:, t, :])
         ident = keep.tile([P, P], F32, name="ident")
         make_identity(nc, ident[:])
 
         def deal(copy, dst, raw, m0, m1):
             copy(
                 dst[:, :, m0:m1, :].rearrange("p t m j -> p m j t"),
-                raw[:].rearrange("p j (m t) -> p m j t", t=PACK),
+                raw.rearrange("p j (m t) -> p m j t", t=PACK),
             )
 
         def w_tiles(name):
@@ -96,7 +106,8 @@ def tile_picked_ycryoem_filt_p_kernel(
         nc.vector.tensor_copy(xs[:], xs_tab[:].indirect(offs_sb[:]))
         w1q = [w_tiles("w1a"), w_tiles("w1b")]
         dealt = ring.tile([P, PACK, P, PACK], BF16, name="dealt", tag="dealt", align_bytes=64)
-        deal(nc.scalar.copy, dealt, w1a_raw, 0, P)
+        for m0 in (0, P // 2):
+            deal(nc.scalar.copy, dealt, w1a_raw[:, :, PACK * m0 : PACK * (m0 + P // 2)], m0, m0 + P // 2)
         quantise(w1q[0], dealt, 0, PACK)
         w2a_raw = keep.tile([P, PACK, H], F32, name="w2a_raw", tag="wraw")
         nc.sync.dma_start(w2a_raw[:], rows(w2, 0))
@@ -133,32 +144,44 @@ def tile_picked_ycryoem_filt_p_kernel(
                 mx_pass(re_ps[t, h], w1q, 0, t, h)
 
         dealt = ring.tile([P, PACK, P, PACK], BF16, name="dealt", tag="dealt", align_bytes=64)
-        deal(nc.scalar.copy, dealt, w1b_raw[0], 0, P // 2)
-        deal(nc.vector.tensor_copy, dealt, w1b_raw[1], P // 2, P)
+        for raw, (m0, m1) in zip(w1b_raw, W1B_PIECES):
+            deal(nc.scalar.copy, dealt, raw[:], m0, m1)
 
         re = [keep.tile([P, S], F32, name="re%d" % t) for t in range(PACK)]
-        ra = [keep.tile([P, 2, PACK, CH], F32, name="ra%d" % h) for h in range(2)]
-        gim = [keep.tile([P, 2, PACK, CH], F32, name="gim%d" % h) for h in range(2)]
-
-        def make_ra(t, h):
-            nc.vector.tensor_tensor(
-                ra[h][:, :, t, :],
-                re_ps[t, h][:].rearrange("p (q c) -> p q c", q=2),
-                ctf_sb[t][:, h * HALF : (h + 1) * HALF].rearrange("p (q c) -> p q c", q=2),
-                MULT,
-            )
-
+        ra = [keep.tile([P, PACK, HALF], F32, name="ra%d" % h) for h in range(2)]
+        gim = [keep.tile([P, PACK, HALF], F32, name="gim%d" % h) for h in range(2)]
+        fil = [keep.tile([P, PACK, HALF], F32, name="fil%d" % h) for h in range(2)]
         rb = {}
 
-        def make_rb(q, t):
-            if t == 0:
-                rb[q] = ring.tile([P, PACK, CH], F32, name="rb", tag="rb")
-            nc.vector.tensor_tensor(
-                rb[q][:, t, :],
-                re[t][:].indirect(half_sb[:, q * (CH // 16) : (q + 1) * (CH // 16)]),
-                ctf_sb[t][:, q * CH : (q + 1) * CH],
-                MULT,
-            )
+        def cols(h):
+            return slice(h * HALF, (h + 1) * HALF)
+
+        def partners(t, h):
+            return re[t][:].indirect(half_sb[:, h * (HALF // 16) : (h + 1) * (HALF // 16)])
+
+        done_ra = set()
+
+        def make_ra(t, h):
+            done_ra.add((t, h))
+            nc.vector.tensor_tensor(ra[h][:, t, :], re_ps[t, h][:], ctf_sb[t][:, cols(h)], MULT)
+
+        def early_ra(q):
+            h, u = divmod(q, 2)
+            for t in (2 * u, 2 * u + 1):
+                make_ra(t, h)
+
+        def apply_ctf(q):
+            h, u = divmod(q, 2)
+            rb[q] = ring.tile([P, 2, HALF], F32, name="rb", tag="rb")
+            for t in (2 * u, 2 * u + 1):
+                if (t, h) not in done_ra:
+                    make_ra(t, h)
+                if (t, h) in SCALAR_FETCHES:
+                    ah = ring.tile([P, HALF], F32, name="ah", tag="ah")
+                    nc.scalar.activation(ah[:], partners(t, h), ACT.Copy)
+                    nc.vector.tensor_tensor(rb[q][:, t % 2, :], ah[:], ctf_sb[t][:, cols(h)], MULT)
+                else:
+                    nc.vector.tensor_tensor(rb[q][:, t % 2, :], partners(t, h), ctf_sb[t][:, cols(h)], MULT)
 
         for t in range(PACK):
             quantise(w1q[1], dealt, t, t + 1)
@@ -166,11 +189,9 @@ def tile_picked_ycryoem_filt_p_kernel(
             for h in range(2):
                 mx_pass(re_ps[t, h], w1q, 1, t, h)
                 nc.scalar.copy(re[t][:, h * HALF : (h + 1) * HALF], re_ps[t, h][:])
-            make_ra(t, 0)
-            make_rb(0, t)
 
         def ra_chunk(q):
-            return ra[q // 2][:, q % 2]
+            return ra[q // 2][:, 2 * (q % 2) : 2 * (q % 2) + 2, :]
 
         def pairs_in(x):
             return x.rearrange("p t (v a b) -> p (t v) a b", a=2, b=2)
@@ -197,7 +218,7 @@ def tile_picked_ycryoem_filt_p_kernel(
         def power_a(q):
             pa = ring.tile([P, 2, PACK * V, 2], F32, name="pa", tag="pa")
             nc.scalar.activation(pairs_out(pa), pairs_in(ra_chunk(q)), ACT.Square)
-            e_ps[q] = bank(2 * (q % 2), "e_ps")
+            e_ps[q] = bank(2 * q, "e_ps")
             shell_sum(e_ps[q][:, 0:CH], pa)
 
         def power_b(q):
@@ -208,10 +229,11 @@ def tile_picked_ycryoem_filt_p_kernel(
         def cross(q):
             xc = ring.tile([P, 2, PACK * V, 2], F32, name="xc", tag="xc")
             nc.vector.tensor_tensor(pairs_out(xc), pairs_in(ra_chunk(q)), pairs_in(rb[q][:]), MULT)
-            n_ps[q] = bank(2 * (q % 2) + 1, "n_ps")
+            n_ps[q] = bank(2 * q + 1, "n_ps")
             shell_sum(n_ps[q][:, 0:CH], xc)
 
         small = {}
+        w_ps = {}
 
         def weight_1(q):
             rs = ring.tile([P, 2 * CH], F32, name="rs", tag="rs")
@@ -232,29 +254,26 @@ def tile_picked_ycryoem_filt_p_kernel(
             nc.vector.scalar_tensor_tensor(top[:], fsc[:], 0.6, z[:], ADD, MULT)
             wien = ring.tile([P, CH], F32, name="wien", tag="wien")
             nc.vector.scalar_tensor_tensor(wien[:], top[:], 0.0, z[:], MAX, MULT)
+            w_ps[q] = bank(2 * q, "w_ps")
             for u in range(2):
-                nc.tensor.transpose(n_ps[q][:, CH + u * P : CH + (u + 1) * P], wien[:, u * P : (u + 1) * P], ident[:])
+                nc.tensor.transpose(w_ps[q][:, u * P : (u + 1) * P], wien[:, u * P : (u + 1) * P], ident[:])
 
         w2q = [w_tiles("w2a"), w_tiles("w2b")]
 
-        def prep_w2(g, raw):
+        def prep_w2(g, raw, copy):
             d2 = ring.tile([P, PACK, P, PACK], BF16, name="dealt", tag="dealt", align_bytes=64)
-            deal(nc.scalar.copy, d2, raw, 0, P)
+            for m0 in range(0, P, 32):
+                deal(copy, d2, raw[:, :, PACK * m0 : PACK * (m0 + 32)], m0, m0 + 32)
             quantise(w2q[g], d2, 0, PACK)
 
         neg_unit = keep.tile([P, PACK], F32, name="neg_unit")
 
-        def second_product(h):
-            for t in range(PACK):
-                acc = bank(4 + t, "im_ps")
+        def second_product(h, ts=range(PACK)):
+            for t in ts:
+                acc = bank(IM_BANKS[h][t], "im_ps")
                 for g in range(PASSES):
                     mx_pass(acc, w2q, g, t, h)
-                nc.scalar.activation(
-                    gim[h][:, :, t, :],
-                    acc[:].rearrange("p (q c) -> p q c", q=2),
-                    ACT.Copy,
-                    scale=neg_unit[:, t : t + 1],
-                )
+                nc.scalar.activation(gim[h][:, t, :], acc[:], ACT.Copy, scale=neg_unit[:, t : t + 1])
 
         w3_codes = keep.tile([P, N], U32, name="w3_codes", align_bytes=64)
         w3_scales = keep.tile([P, N], U8, name="w3_scales", align_bytes=64)
@@ -269,34 +288,39 @@ def tile_picked_ycryoem_filt_p_kernel(
 
         hid = {}
 
-        def make_hid(q):
-            fil = ring.tile([P, PACK, CH], F32, name="fil", tag="fil")
-            for t in range(PACK):
+        def filter_a(q):
+            h, u = divmod(q, 2)
+            for t in (2 * u, 2 * u + 1):
                 nc.vector.scalar_tensor_tensor(
-                    fil[:, t, :].rearrange("p (v d) -> p v d", d=D),
-                    n_ps[q][:, CH + t * V : CH + (t + 1) * V].unsqueeze(2).to_broadcast([P, V, D]),
+                    fil[h][:, t, :].rearrange("p (v d) -> p v d", d=D),
+                    w_ps[q][:, (t % 2) * P : (t % 2 + 1) * P].unsqueeze(2).to_broadcast([P, P, D]),
                     unit_sb[:, t : t + 1],
-                    ra_chunk(q)[:, t, :].rearrange("p (v d) -> p v d", d=D),
+                    ra[h][:, t, :].rearrange("p (v d) -> p v d", d=D),
                     MULT,
                     MULT,
                 )
-            hid[q] = ring.tile([P, CH, PACK], BF16, name="hid", tag="hid", align_bytes=64)
+
+        def make_hid(n):
+            h, c0, c1 = HID_PIECES[n]
+            hid[n] = ring.tile([P, c1 - c0, PACK], BF16, name="hid", tag="hid", align_bytes=64)
             nc.vector.tensor_tensor(
-                hid[q][:].rearrange("p (c i) t -> p c t i", i=4),
-                fil[:].rearrange("p t (c i) -> p c t i", i=4),
-                gim[q // 2][:, q % 2].rearrange("p t (c i) -> p c t i", i=4),
+                hid[n][:].rearrange("p (c i) t -> p c t i", i=4),
+                fil[h][:, :, c0:c1].rearrange("p t (c i) -> p c t i", i=4),
+                gim[h][:, :, c0:c1].rearrange("p t (c i) -> p c t i", i=4),
                 ADD,
             )
 
-        def finish(q):
-            codes = ring.tile([P, CH], U32, name="hid_codes", tag="hid_codes", align_bytes=64)
-            scales = ring.tile([P, CH], U8, name="hid_scales", tag="hid_scales", align_bytes=64)
+        def finish(n):
+            h, c0, c1 = HID_PIECES[n]
+            width = c1 - c0
+            codes = ring.tile([P, width], U32, name="hid_codes", tag="hid_codes", align_bytes=64)
+            scales = ring.tile([P, width], U8, name="hid_scales", tag="hid_scales", align_bytes=64)
             nc.vector.quantize_mx(
-                out=codes[:].bitcast(FP8X4), scales=scales[:], in_=hid[q][:].rearrange("p c t -> p (c t)")
+                out=codes[:].bitcast(FP8X4), scales=scales[:], in_=hid[n][:].rearrange("p c t -> p (c t)")
             )
-            acc = bank(4 + q, "out_ps")
+            acc = bank(OUT_BANKS[n], "out_ps")
             nc.tensor.matmul_mx(
-                out=acc[:, 0:CH],
+                out=acc[:, 0:width],
                 lhsT=w3_codes[:].bitcast(FP8X4),
                 lhsT_scale=w3_scales[:],
                 rhs=codes[:].bitcast(FP8X4),
@@ -304,49 +328,50 @@ def tile_picked_ycryoem_filt_p_kernel(
                 start=True,
                 stop=True,
             )
-            res = ring.tile([P, CH], F32, name="res", tag="res")
-            nc.scalar.copy(res[:], acc[:, 0:CH])
-            nc.sync.dma_start(out[:, q * CH : (q + 1) * CH], res[:])
+            res = ring.tile([P, width], F32, name="res", tag="res", bufs=3)
+            nc.scalar.copy(res[:], acc[:, 0:width])
+            nc.sync.dma_start(out[:, h * HALF + c0 : h * HALF + c1], res[:])
 
-        def gathers(q):
-            for t in range(PACK):
-                make_rb(q, t)
-
+        apply_ctf(0)
         power_a(0)
         power_b(0)
         cross(0)
-        gathers(1)
+        prep_w2(0, w2a_raw, nc.vector.tensor_copy)
+        apply_ctf(1)
         power_a(1)
         power_b(1)
         cross(1)
-        for t in range(PACK):
-            make_ra(t, 1)
         weight_1(0)
-        prep_w2(0, w2a_raw)
-        prep_w2(1, w2b_raw)
-        prep_w3()
-        gathers(2)
         weight_2(0)
-        second_product(0)
-        weight_1(1)
+        apply_ctf(2)
         power_a(2)
         power_b(2)
-        weight_2(1)
-        make_hid(0)
         cross(2)
-        gathers(3)
-        second_product(1)
-        finish(0)
-        weight_1(2)
+        weight_1(1)
+        weight_2(1)
+        apply_ctf(3)
         power_a(3)
         power_b(3)
-        make_hid(1)
         cross(3)
+        weight_1(2)
+        prep_w2(1, w2b_raw, nc.scalar.copy)
+        prep_w3()
         weight_2(2)
-        finish(1)
+        second_product(0)
+        second_product(1)
         weight_1(3)
-        make_hid(2)
         weight_2(3)
-        finish(2)
+        filter_a(0)
+        filter_a(1)
+        make_hid(0)
+        make_hid(1)
+        finish(0)
+        filter_a(2)
+        finish(1)
+        filter_a(3)
+        make_hid(2)
         make_hid(3)
+        finish(2)
+        make_hid(4)
         finish(3)
+        finish(4)

@@ -193,44 +193,45 @@ def tile_picked_ycryoem_filt_p_kernel(
         def ra_chunk(q):
             return ra[q // 2][:, 2 * (q % 2) : 2 * (q % 2) + 2, :]
 
-        def pairs_in(x):
-            return x.rearrange("p t (v a b) -> p (t v) a b", a=2, b=2)
-
-        def pairs_out(x):
-            return x[:].rearrange("p a w b -> p w a b")
-
-        def shell_sum(dst, src):
+        def shell_sum(dst, members):
             for u in range(2):
-                for a in range(2):
-                    for b in range(2):
-                        nc.tensor.matmul(
-                            dst[:, u * P : (u + 1) * P],
-                            src[:, a, u * P : (u + 1) * P, b],
-                            ident[:],
-                            start=(a == 0 and b == 0),
-                            stop=(a == 1 and b == 1),
-                            is_transpose=True,
-                        )
+                for d in range(D):
+                    nc.tensor.matmul(
+                        dst[:, u * P : (u + 1) * P],
+                        members(d)[:, u * P : (u + 1) * P],
+                        ident[:],
+                        start=(d == 0),
+                        stop=(d == D - 1),
+                        is_transpose=True,
+                    )
 
         e_ps = {}
         n_ps = {}
 
+        def square_and_sum(dst, src, name):
+            sq = ring.tile([P, D, CH], F32, name=name, tag=name)
+            nc.scalar.activation(
+                sq[:].rearrange("p d w -> p w d"), src.rearrange("p t (v d) -> p (t v) d", d=D), ACT.Square
+            )
+            shell_sum(dst, lambda d: sq[:, d, :])
+
         def power_a(q):
-            pa = ring.tile([P, 2, PACK * V, 2], F32, name="pa", tag="pa")
-            nc.scalar.activation(pairs_out(pa), pairs_in(ra_chunk(q)), ACT.Square)
             e_ps[q] = bank(2 * q, "e_ps")
-            shell_sum(e_ps[q][:, 0:CH], pa)
+            square_and_sum(e_ps[q][:, 0:CH], ra_chunk(q), "pa")
 
         def power_b(q):
-            pb = ring.tile([P, 2, PACK * V, 2], F32, name="pb", tag="pb")
-            nc.scalar.activation(pairs_out(pb), pairs_in(rb[q][:]), ACT.Square)
-            shell_sum(e_ps[q][:, CH : 2 * CH], pb)
+            square_and_sum(e_ps[q][:, CH : 2 * CH], rb[q][:], "pb")
 
         def cross(q):
-            xc = ring.tile([P, 2, PACK * V, 2], F32, name="xc", tag="xc")
-            nc.vector.tensor_tensor(pairs_out(xc), pairs_in(ra_chunk(q)), pairs_in(rb[q][:]), MULT)
+            xc = ring.tile([P, D, CH], F32, name="xc", tag="xc")
+            nc.vector.tensor_tensor(
+                xc[:].rearrange("p d w -> p w d"),
+                ra_chunk(q).rearrange("p t (v d) -> p (t v) d", d=D),
+                rb[q][:].rearrange("p t (v d) -> p (t v) d", d=D),
+                MULT,
+            )
             n_ps[q] = bank(2 * q + 1, "n_ps")
-            shell_sum(n_ps[q][:, 0:CH], xc)
+            shell_sum(n_ps[q][:, 0:CH], lambda d: xc[:, d, :])
 
         small = {}
         w_ps = {}

@@ -20,16 +20,21 @@ MAX = mybir.AluOpType.max
 
 P = 128
 PACK = 4
-PASSES = K // (P * PACK)
+K_PASS = P * PACK
+PASSES = K // K_PASS
+QUADRANT = 32
+LIST_COL = 16
+BANK = 512
 HALF = S // 2
-CH = S // 4
-NCH = S // CH
-V = CH // D
-SCALAR_FETCHES = ((3, 0), (1, 1), (3, 1))
-IM_BANKS = ((1, 3, 1, 3), (1, 3, 1, 3))
+CHUNKS = 4
+SUMS = 2 * HALF // D
+LAST = CHUNKS - 1
+
+W1_LAST_PIECES = ((0, 64), (64, 96), (96, 128))
+W2_PIECE = 32
+SCALAR_TILE = 3
 HID_PIECES = ((0, 0, 256), (0, 256, 512), (1, 0, 256), (1, 256, 384), (1, 384, 512))
-OUT_BANKS = (0, 2, 4, 6, 0)
-W1B_PIECES = ((0, 64), (64, 96), (96, 128))
+IM_BANKS = (1, 3, 5)
 
 
 def tile_picked_ycryoem_filt_p_kernel(
@@ -42,97 +47,107 @@ def tile_picked_ycryoem_filt_p_kernel(
         psum = ctx.enter_context(tc.psum_pool(name="psum", bufs=1))
 
         def bank(b, name):
-            return psum.tile([P, 512], F32, name=name, tag="bank%d" % b)
+            return psum.tile([P, BANK], F32, name=name, tag="bank%d" % b)
 
-        offs_sb = keep.tile([P, S // 16], U16, name="offs_sb")
-        half_sb = keep.tile([P, S // 16], U16, name="half_sb")
-        xs_tab = keep.tile([P, T], U8, name="xs_tab", align_bytes=64)
-        nc.vector.memset(xs_tab[:].bitcast(I32), 0)
+        def pass_rows(w, g):
+            return w[g * K_PASS : (g + 1) * K_PASS, :].rearrange("(p j) c -> p j c", j=PACK)
+
+        def cols(h):
+            return slice(h * HALF, (h + 1) * HALF)
+
+        def entries(lst, h):
+            return lst[:, h * HALF // LIST_COL : (h + 1) * HALF // LIST_COL]
+
+        offs_sb = keep.tile([P, S // LIST_COL], U16, name="offs_sb")
+        half_sb = keep.tile([P, S // LIST_COL], U16, name="half_sb")
+        scale_table = keep.tile([P, T], U8, name="scale_table", align_bytes=64)
+        nc.vector.memset(scale_table[:].bitcast(I32), 0)
         nc.sync.dma_start(offs_sb[:], offs)
+        scale_rows = keep.tile([P, T // 4], I32, name="scale_rows")
+        for r in range(P // QUADRANT):
+            live = slice(QUADRANT * r, QUADRANT * r + 4 * PASSES)
+            nc.sync.dma_start(scale_rows[live, :], x_scales[:, 4 * r : 4 * r + 4, :].bitcast(I32))
+            nc.vector.tensor_copy(scale_table[live, :].bitcast(I32), scale_rows[live, :])
 
-        def rows(w, g):
-            return w[g * 512 : (g + 1) * 512, :].rearrange("(p j) c -> p j c", j=PACK)
-
-        xs_rows = keep.tile([P, T // 4], I32, name="xs_rows")
-        for q in range(4):
-            live = slice(32 * q, 32 * q + 4 * PASSES)
-            nc.sync.dma_start(xs_rows[live, :], x_scales[:, 4 * q : 4 * q + 4, :].bitcast(I32))
-            nc.vector.tensor_copy(xs_tab[live, :].bitcast(I32), xs_rows[live, :])
-        w1a_raw = keep.tile([P, PACK, H], F32, name="w1a_raw", tag="wraw")
-        for c0 in (0, H // 2):
-            nc.sync.dma_start(w1a_raw[:, :, c0 : c0 + H // 2], rows(w1, 0)[:, :, c0 : c0 + H // 2])
-        xw_tab = [keep.tile([P, T], I32, name="xw_tab%d" % g, align_bytes=64) for g in range(PASSES)]
-        w1b_raw = [keep.tile([P, PACK, PACK * (m1 - m0)], F32, name="w1b_raw%d" % m0) for m0, m1 in W1B_PIECES]
+        w1_first = keep.tile([P, PACK, H], F32, name="w1_first", tag="first_pass")
+        nc.sync.dma_start(w1_first[:], pass_rows(w1, 0))
+        word_table = [keep.tile([P, T], I32, name="word_table%d" % g, align_bytes=64) for g in range(PASSES)]
+        w1_last = [keep.tile([P, PACK, PACK * (m1 - m0)], F32, name="w1_last%d" % m0) for m0, m1 in W1_LAST_PIECES]
 
         def load_words(g):
-            nc.sync.dma_start(xw_tab[g][:], x_words[g].rearrange("p n t -> p (n t)").bitcast(I32))
+            nc.sync.dma_start(word_table[g][:], x_words[g].rearrange("p n t -> p (n t)").bitcast(I32))
 
-        def load_w1b(n):
-            m0, m1 = W1B_PIECES[n]
-            nc.sync.dma_start(w1b_raw[n][:], rows(w1, 1)[:, :, PACK * m0 : PACK * m1])
+        def load_w1_last(n):
+            m0, m1 = W1_LAST_PIECES[n]
+            nc.sync.dma_start(w1_last[n][:], pass_rows(w1, 1)[:, :, PACK * m0 : PACK * m1])
 
         load_words(0)
-        load_w1b(0)
+        load_w1_last(0)
         load_words(1)
-        load_w1b(1)
-        load_w1b(2)
+        load_w1_last(1)
+        load_w1_last(2)
         nc.sync.dma_start(half_sb[:], half)
-        ctf_all = keep.tile([P, PACK, S], F32, name="ctf_all")
-        ctf_sb = [ctf_all[:, t, :] for t in range(PACK)]
-        for t in range(PACK):
-            nc.sync.dma_start(ctf_sb[t], ctf.rearrange("(p t) j -> p t j", t=PACK)[:, t, :])
+        ctf_sb = keep.tile([P, PACK, S], F32, name="ctf_sb")
         ident = keep.tile([P, P], F32, name="ident")
         make_identity(nc, ident[:])
+        table_warm = keep.tile([P, 1], F32, name="table_warm")
+        nc.scalar.activation(table_warm[:], ident[:, 0:1], ACT.Abs_reciprocal_sqrt, bias=1.0)
 
-        def deal(copy, dst, raw, m0, m1):
+        def new_dealt():
+            return ring.tile([P, PACK, P, PACK], BF16, name="dealt", tag="dealt", align_bytes=64)
+
+        def deal(copy, dealt, raw, m0, m1):
             copy(
-                dst[:, :, m0:m1, :].rearrange("p t m j -> p m j t"),
+                dealt[:, :, m0:m1, :].rearrange("p t m j -> p m j t"),
                 raw.rearrange("p j (m t) -> p m j t", t=PACK),
             )
 
-        def w_tiles(name):
+        def weight_planes(name):
             codes = keep.tile([P, H], U32, name=name + "_codes", align_bytes=64)
             scales = keep.tile([P, H], U8, name=name + "_scales", align_bytes=64)
             return codes, scales
 
-        def quantise(wq, dealt, t0, t1):
+        def quantise(planes, dealt, t0, t1):
             nc.vector.quantize_mx(
-                out=wq[0][:, t0 * P : t1 * P].bitcast(FP8X4),
-                scales=wq[1][:, t0 * P : t1 * P],
+                out=planes[0][:, t0 * P : t1 * P].bitcast(FP8X4),
+                scales=planes[1][:, t0 * P : t1 * P],
                 in_=dealt[:, t0:t1].rearrange("p t m j -> p (t m j)"),
             )
 
-        xs = keep.tile([P, S], U8, name="xs", align_bytes=64)
-        nc.vector.tensor_copy(xs[:], xs_tab[:].indirect(offs_sb[:]))
-        w1q = [w_tiles("w1a"), w_tiles("w1b")]
-        dealt = ring.tile([P, PACK, P, PACK], BF16, name="dealt", tag="dealt", align_bytes=64)
+        x_scale = keep.tile([P, S], U8, name="x_scale", align_bytes=64)
+        nc.vector.tensor_copy(x_scale[:], scale_table[:].indirect(offs_sb[:]))
+        w1_planes = [weight_planes("w1_pass%d" % g) for g in range(PASSES)]
+        dealt = new_dealt()
         for m0 in (0, P // 2):
-            deal(nc.scalar.copy, dealt, w1a_raw[:, :, PACK * m0 : PACK * (m0 + P // 2)], m0, m0 + P // 2)
-        quantise(w1q[0], dealt, 0, PACK)
-        w2a_raw = keep.tile([P, PACK, H], F32, name="w2a_raw", tag="wraw")
-        nc.sync.dma_start(w2a_raw[:], rows(w2, 0))
-        w2b_raw = keep.tile([P, PACK, H], F32, name="w2b_raw")
-        nc.sync.dma_start(w2b_raw[:], rows(w2, 1))
+            deal(nc.scalar.copy, dealt, w1_first[:, :, PACK * m0 : PACK * (m0 + P // 2)], m0, m0 + P // 2)
+        quantise(w1_planes[0], dealt, 0, PACK)
+
+        w2_raw = [
+            keep.tile([P, PACK, H], F32, name="w2_first", tag="first_pass"),
+            keep.tile([P, PACK, H], F32, name="w2_last"),
+        ]
+        for t in range(PACK):
+            nc.sync.dma_start(ctf_sb[:, t, :], ctf.rearrange("(p t) j -> p t j", t=PACK)[:, t, :])
+        for g in range(PASSES):
+            nc.sync.dma_start(w2_raw[g][:], pass_rows(w2, g))
         unit_sb = keep.tile([P, PACK], F32, name="unit_sb")
         nc.sync.dma_start(unit_sb[:], unit.rearrange("(p t) o -> p (t o)", t=PACK))
         w3_raw = keep.tile([P, PACK, N], F32, name="w3_raw")
-        nc.sync.dma_start(w3_raw[:], rows(w3, 0))
+        nc.sync.dma_start(w3_raw[:], pass_rows(w3, 0))
 
-        xw = {}
+        x_code = {}
         for g in range(PASSES):
             for h in range(2):
-                xw[g, h] = keep.tile([P, HALF], U32, name="xw%d%d" % (g, h), align_bytes=64)
-                nc.vector.tensor_copy(
-                    xw[g, h][:], xw_tab[g][:].bitcast(U32).indirect(offs_sb[:, h * 32 : (h + 1) * 32])
-                )
+                x_code[g, h] = keep.tile([P, HALF], U32, name="x_code%d%d" % (g, h), align_bytes=64)
+                nc.vector.tensor_copy(x_code[g, h][:], word_table[g][:].bitcast(U32).indirect(entries(offs_sb, h)))
 
-        def mx_pass(acc, wq, g, t, h):
+        def mx_pass(acc, planes, g, t, h):
             nc.tensor.matmul_mx(
                 out=acc[:],
-                lhsT=wq[g][0][:, t * P : (t + 1) * P].bitcast(FP8X4),
-                lhsT_scale=wq[g][1][:, t * P : (t + 1) * P],
-                rhs=xw[g, h][:].bitcast(FP8X4),
-                rhs_scale=xs[4 * g : P, h * HALF : (h + 1) * HALF],
+                lhsT=planes[g][0][:, t * P : (t + 1) * P].bitcast(FP8X4),
+                lhsT_scale=planes[g][1][:, t * P : (t + 1) * P],
+                rhs=x_code[g, h][:].bitcast(FP8X4),
+                rhs_scale=x_scale[4 * g : P, cols(h)],
                 start=(g == 0),
                 stop=(g == PASSES - 1),
             )
@@ -140,161 +155,142 @@ def tile_picked_ycryoem_filt_p_kernel(
         re_ps = {}
         for h in range(2):
             for t in range(PACK):
-                re_ps[t, h] = bank(4 * h + t, "re_ps")
-                mx_pass(re_ps[t, h], w1q, 0, t, h)
+                re_ps[t, h] = bank(PACK * h + t, "re_ps")
+                mx_pass(re_ps[t, h], w1_planes, 0, t, h)
 
-        dealt = ring.tile([P, PACK, P, PACK], BF16, name="dealt", tag="dealt", align_bytes=64)
-        for raw, (m0, m1) in zip(w1b_raw, W1B_PIECES):
+        dealt = new_dealt()
+        for raw, (m0, m1) in zip(w1_last, W1_LAST_PIECES):
             deal(nc.scalar.copy, dealt, raw[:], m0, m1)
+        for t in range(PACK):
+            quantise(w1_planes[1], dealt, t, t + 1)
 
         re = [keep.tile([P, S], F32, name="re%d" % t) for t in range(PACK)]
-        ra = [keep.tile([P, PACK, HALF], F32, name="ra%d" % h) for h in range(2)]
-        gim = [keep.tile([P, PACK, HALF], F32, name="gim%d" % h) for h in range(2)]
-        fil = [keep.tile([P, PACK, HALF], F32, name="fil%d" % h) for h in range(2)]
-        rb = {}
-
-        def cols(h):
-            return slice(h * HALF, (h + 1) * HALF)
-
-        def partners(t, h):
-            return re[t][:].indirect(half_sb[:, h * (HALF // 16) : (h + 1) * (HALF // 16)])
-
-        done_ra = set()
-
-        def make_ra(t, h):
-            done_ra.add((t, h))
-            nc.vector.tensor_tensor(ra[h][:, t, :], re_ps[t, h][:], ctf_sb[t][:, cols(h)], MULT)
-
-        def early_ra(q):
-            h, u = divmod(q, 2)
-            for t in (2 * u, 2 * u + 1):
-                make_ra(t, h)
-
-        def apply_ctf(q):
-            h, u = divmod(q, 2)
-            rb[q] = ring.tile([P, 2, HALF], F32, name="rb", tag="rb")
-            for t in (2 * u, 2 * u + 1):
-                if (t, h) not in done_ra:
-                    make_ra(t, h)
-                if (t, h) in SCALAR_FETCHES:
-                    ah = ring.tile([P, HALF], F32, name="ah", tag="ah")
-                    nc.scalar.activation(ah[:], partners(t, h), ACT.Copy)
-                    nc.vector.tensor_tensor(rb[q][:, t % 2, :], ah[:], ctf_sb[t][:, cols(h)], MULT)
-                else:
-                    nc.vector.tensor_tensor(rb[q][:, t % 2, :], partners(t, h), ctf_sb[t][:, cols(h)], MULT)
-
-        for t in range(PACK):
-            quantise(w1q[1], dealt, t, t + 1)
         for t in range(PACK):
             for h in range(2):
-                mx_pass(re_ps[t, h], w1q, 1, t, h)
-                nc.scalar.copy(re[t][:, h * HALF : (h + 1) * HALF], re_ps[t, h][:])
+                mx_pass(re_ps[t, h], w1_planes, 1, t, h)
+                nc.scalar.copy(re[t][:, cols(h)], re_ps[t, h][:])
 
-        def ra_chunk(q):
-            return ra[q // 2][:, 2 * (q % 2) : 2 * (q % 2) + 2, :]
+        ra = [keep.tile([P, PACK, HALF], F32, name="ra%d" % h) for h in range(2)]
+        im_term = [keep.tile([P, PACK, HALF], F32, name="im_term%d" % h) for h in range(2)]
+        ra_term = [keep.tile([P, PACK, HALF], F32, name="ra_term%d" % h) for h in range(2)]
+        squares_ps, cross_ps, wien_ps, factors, hid = {}, {}, {}, {}, {}
+
+        def chunk_tiles(q):
+            return (2 * (q % 2), 2 * (q % 2) + 1)
+
+        def new_members(name):
+            return ring.tile([P, 2, SUMS, 2], F32, name=name, tag=name)
+
+        def as_written(members):
+            return members[:].rearrange("p a w b -> p w a b")
+
+        def by_member(x):
+            return x.rearrange("p t (v a b) -> p (t v) a b", a=2, b=2)
 
         def shell_sum(dst, members):
             for u in range(2):
                 for d in range(D):
                     nc.tensor.matmul(
                         dst[:, u * P : (u + 1) * P],
-                        members(d)[:, u * P : (u + 1) * P],
+                        members[:, d // 2, u * P : (u + 1) * P, d % 2],
                         ident[:],
                         start=(d == 0),
                         stop=(d == D - 1),
                         is_transpose=True,
                     )
 
-        e_ps = {}
-        n_ps = {}
+        def correlate(q):
+            h = q // 2
+            rb = ring.tile([P, 2, HALF], F32, name="rb", tag="rb")
+            for t in chunk_tiles(q):
+                nc.vector.tensor_tensor(ra[h][:, t, :], re_ps[t, h][:], ctf_sb[:, t, cols(h)], MULT)
+                partner = re[t][:].indirect(entries(half_sb, h))
+                if t == SCALAR_TILE:
+                    ah = ring.tile([P, HALF], F32, name="ah", tag="ah")
+                    nc.scalar.activation(ah[:], partner, ACT.Copy)
+                    partner = ah[:]
+                nc.vector.tensor_tensor(rb[:, t % 2, :], partner, ctf_sb[:, t, cols(h)], MULT)
+            t0, t1 = chunk_tiles(q)
+            ra_q = ra[h][:, t0 : t1 + 1, :]
+            pa = new_members("pa")
+            nc.scalar.activation(as_written(pa), by_member(ra_q), ACT.Square)
+            squares_ps[q] = bank(2 * q, "squares_ps")
+            shell_sum(squares_ps[q][:, 0:SUMS], pa)
+            pb = new_members("pb")
+            nc.scalar.activation(as_written(pb), by_member(rb[:]), ACT.Square)
+            shell_sum(squares_ps[q][:, SUMS : 2 * SUMS], pb)
+            xc = new_members("xc")
+            nc.vector.tensor_tensor(as_written(xc), by_member(ra_q), by_member(rb[:]), MULT)
+            cross_ps[q] = bank(2 * q + 1, "cross_ps")
+            shell_sum(cross_ps[q][:, 0:SUMS], xc)
 
-        def square_and_sum(dst, src, name):
-            sq = ring.tile([P, D, CH], F32, name=name, tag=name)
-            nc.scalar.activation(
-                sq[:].rearrange("p d w -> p w d"), src.rearrange("p t (v d) -> p (t v) d", d=D), ACT.Square
-            )
-            shell_sum(dst, lambda d: sq[:, d, :])
+        def small(name):
+            return ring.tile([P, SUMS], F32, name=name, tag=name)
 
-        def power_a(q):
-            e_ps[q] = bank(2 * q, "e_ps")
-            square_and_sum(e_ps[q][:, 0:CH], ra_chunk(q), "pa")
-
-        def power_b(q):
-            square_and_sum(e_ps[q][:, CH : 2 * CH], rb[q][:], "pb")
-
-        def cross(q):
-            xc = ring.tile([P, D, CH], F32, name="xc", tag="xc")
-            nc.vector.tensor_tensor(
-                xc[:].rearrange("p d w -> p w d"),
-                ra_chunk(q).rearrange("p t (v d) -> p (t v) d", d=D),
-                rb[q][:].rearrange("p t (v d) -> p (t v) d", d=D),
-                MULT,
-            )
-            n_ps[q] = bank(2 * q + 1, "n_ps")
-            shell_sum(n_ps[q][:, 0:CH], lambda d: xc[:, d, :])
-
-        small = {}
-        w_ps = {}
-
-        def weight_1(q):
-            rs = ring.tile([P, 2 * CH], F32, name="rs", tag="rs")
-            nc.scalar.activation(rs[:], e_ps[q][:], ACT.Abs_reciprocal_sqrt, bias=0.3)
-            f1 = ring.tile([P, CH], F32, name="f1", tag="f1")
-            nc.vector.tensor_tensor(f1[:], n_ps[q][:, 0:CH], rs[:, 0:CH], MULT)
-            fsc = ring.tile([P, CH], F32, name="fsc", tag="fsc")
-            nc.vector.tensor_tensor(fsc[:], f1[:], rs[:, CH : 2 * CH], MULT)
-            mag = ring.tile([P, CH], F32, name="mag", tag="mag")
+        def weight_factors(q):
+            inv = ring.tile([P, 2 * SUMS], F32, name="inv", tag="inv")
+            nc.scalar.activation(inv[:], squares_ps[q][:], ACT.Abs_reciprocal_sqrt, bias=0.3)
+            part = small("part")
+            nc.vector.tensor_tensor(part[:], cross_ps[q][:, 0:SUMS], inv[:, 0:SUMS], MULT)
+            fsc = small("fsc")
+            nc.vector.tensor_tensor(fsc[:], part[:], inv[:, SUMS : 2 * SUMS], MULT)
+            mag = small("mag")
             nc.scalar.activation(mag[:], fsc[:], ACT.Abs)
-            z = ring.tile([P, CH], F32, name="z", tag="z")
-            nc.scalar.activation(z[:], mag[:], ACT.Abs_reciprocal_sqrt, bias=0.5)
-            small[q] = (fsc, z)
+            root = small("root")
+            nc.scalar.activation(root[:], mag[:], ACT.Abs_reciprocal_sqrt, bias=0.5)
+            factors[q] = (fsc, root)
+            if q == LAST:
+                recip = small("recip")
+                top = small("top")
+                nc.scalar.activation(top[:], fsc[:], ACT.Relu, bias=0.6)
+                nc.scalar.activation(recip[:], root[:], ACT.Square)
+                factors[q] = (top, recip)
 
-        def weight_2(q):
-            fsc, z = small[q]
-            top = ring.tile([P, CH], F32, name="top", tag="top")
-            nc.vector.scalar_tensor_tensor(top[:], fsc[:], 0.6, z[:], ADD, MULT)
-            wien = ring.tile([P, CH], F32, name="wien", tag="wien")
-            nc.vector.scalar_tensor_tensor(wien[:], top[:], 0.0, z[:], MAX, MULT)
-            w_ps[q] = bank(2 * q, "w_ps")
+        def weight(q):
+            wien = small("wien")
+            if q == LAST:
+                top, recip = factors[q]
+                nc.vector.tensor_tensor(wien[:], top[:], recip[:], MULT)
+            else:
+                fsc, root = factors[q]
+                top = small("top")
+                nc.vector.scalar_tensor_tensor(top[:], fsc[:], 0.6, root[:], ADD, MULT)
+                nc.vector.scalar_tensor_tensor(wien[:], top[:], 0.0, root[:], MAX, MULT)
+            wien_ps[q] = bank(2 * q, "wien_ps")
             for u in range(2):
-                nc.tensor.transpose(w_ps[q][:, u * P : (u + 1) * P], wien[:, u * P : (u + 1) * P], ident[:])
+                nc.tensor.transpose(wien_ps[q][:, u * P : (u + 1) * P], wien[:, u * P : (u + 1) * P], ident[:])
 
-        w2q = [w_tiles("w2a"), w_tiles("w2b")]
-
-        def prep_w2(g, raw, copy):
-            d2 = ring.tile([P, PACK, P, PACK], BF16, name="dealt", tag="dealt", align_bytes=64)
-            for m0 in range(0, P, 32):
-                deal(copy, d2, raw[:, :, PACK * m0 : PACK * (m0 + 32)], m0, m0 + 32)
-            quantise(w2q[g], d2, 0, PACK)
-
-        neg_unit = keep.tile([P, PACK], F32, name="neg_unit")
-
-        def second_product(h, ts=range(PACK)):
-            for t in ts:
-                acc = bank(IM_BANKS[h][t], "im_ps")
-                for g in range(PASSES):
-                    mx_pass(acc, w2q, g, t, h)
-                nc.scalar.activation(gim[h][:, t, :], acc[:], ACT.Copy, scale=neg_unit[:, t : t + 1])
-
+        w2_planes = [weight_planes("w2_pass%d" % g) for g in range(PASSES)]
+        im_scale = keep.tile([P, PACK], F32, name="im_scale")
         w3_codes = keep.tile([P, N], U32, name="w3_codes", align_bytes=64)
         w3_scales = keep.tile([P, N], U8, name="w3_scales", align_bytes=64)
 
-        def prep_w3():
-            nc.vector.tensor_scalar(neg_unit[:], unit_sb[:], -0.4, None, MULT)
-            d3 = keep.tile([P, N, PACK], BF16, name="w3_dealt", align_bytes=64)
-            nc.scalar.copy(d3[:], w3_raw[:].rearrange("p j m -> p m j"))
+        def quantise_w2_w3():
+            for g, copy in enumerate((nc.vector.tensor_copy, nc.scalar.copy)):
+                w2_dealt = new_dealt()
+                for m0 in range(0, P, W2_PIECE):
+                    m1 = m0 + W2_PIECE
+                    deal(copy, w2_dealt, w2_raw[g][:, :, PACK * m0 : PACK * m1], m0, m1)
+                quantise(w2_planes[g], w2_dealt, 0, PACK)
+            nc.vector.tensor_scalar(im_scale[:], unit_sb[:], -0.4, None, MULT)
+            w3_words = keep.tile([P, N, PACK], BF16, name="w3_words", align_bytes=64)
+            nc.scalar.copy(w3_words[:], w3_raw[:].rearrange("p j m -> p m j"))
             nc.vector.quantize_mx(
-                out=w3_codes[:].bitcast(FP8X4), scales=w3_scales[:], in_=d3[:].rearrange("p m j -> p (m j)")
+                out=w3_codes[:].bitcast(FP8X4), scales=w3_scales[:], in_=w3_words[:].rearrange("p m j -> p (m j)")
             )
 
-        hid = {}
+        def second_product(h, t):
+            acc = bank(IM_BANKS[(PACK * h + t) % len(IM_BANKS)], "im_ps")
+            for g in range(PASSES):
+                mx_pass(acc, w2_planes, g, t, h)
+            nc.scalar.activation(im_term[h][:, t, :], acc[:], ACT.Copy, scale=im_scale[:, t : t + 1])
 
-        def filter_a(q):
-            h, u = divmod(q, 2)
-            for t in (2 * u, 2 * u + 1):
+        def apply_weight(q):
+            h = q // 2
+            for t in chunk_tiles(q):
                 nc.vector.scalar_tensor_tensor(
-                    fil[h][:, t, :].rearrange("p (v d) -> p v d", d=D),
-                    w_ps[q][:, (t % 2) * P : (t % 2 + 1) * P].unsqueeze(2).to_broadcast([P, P, D]),
+                    ra_term[h][:, t, :].rearrange("p (v d) -> p v d", d=D),
+                    wien_ps[q][:, (t % 2) * P : (t % 2 + 1) * P].unsqueeze(2).to_broadcast([P, P, D]),
                     unit_sb[:, t : t + 1],
                     ra[h][:, t, :].rearrange("p (v d) -> p v d", d=D),
                     MULT,
@@ -306,12 +302,12 @@ def tile_picked_ycryoem_filt_p_kernel(
             hid[n] = ring.tile([P, c1 - c0, PACK], BF16, name="hid", tag="hid", align_bytes=64)
             nc.vector.tensor_tensor(
                 hid[n][:].rearrange("p (c i) t -> p c t i", i=4),
-                fil[h][:, :, c0:c1].rearrange("p t (c i) -> p c t i", i=4),
-                gim[h][:, :, c0:c1].rearrange("p t (c i) -> p c t i", i=4),
+                ra_term[h][:, :, c0:c1].rearrange("p t (c i) -> p c t i", i=4),
+                im_term[h][:, :, c0:c1].rearrange("p t (c i) -> p c t i", i=4),
                 ADD,
             )
 
-        def finish(n):
+        def last_product(n):
             h, c0, c1 = HID_PIECES[n]
             width = c1 - c0
             codes = ring.tile([P, width], U32, name="hid_codes", tag="hid_codes", align_bytes=64)
@@ -319,7 +315,7 @@ def tile_picked_ycryoem_filt_p_kernel(
             nc.vector.quantize_mx(
                 out=codes[:].bitcast(FP8X4), scales=scales[:], in_=hid[n][:].rearrange("p c t -> p (c t)")
             )
-            acc = bank(OUT_BANKS[n], "out_ps")
+            acc = bank(2 * (n % CHUNKS), "out_ps")
             nc.tensor.matmul_mx(
                 out=acc[:, 0:width],
                 lhsT=w3_codes[:].bitcast(FP8X4),
@@ -333,46 +329,22 @@ def tile_picked_ycryoem_filt_p_kernel(
             nc.scalar.copy(res[:], acc[:, 0:width])
             nc.sync.dma_start(out[:, h * HALF + c0 : h * HALF + c1], res[:])
 
-        apply_ctf(0)
-        power_a(0)
-        power_b(0)
-        cross(0)
-        prep_w2(0, w2a_raw, nc.vector.tensor_copy)
-        apply_ctf(1)
-        power_a(1)
-        power_b(1)
-        cross(1)
-        weight_1(0)
-        weight_2(0)
-        apply_ctf(2)
-        power_a(2)
-        power_b(2)
-        cross(2)
-        weight_1(1)
-        weight_2(1)
-        apply_ctf(3)
-        power_a(3)
-        power_b(3)
-        cross(3)
-        weight_1(2)
-        prep_w2(1, w2b_raw, nc.scalar.copy)
-        prep_w3()
-        weight_2(2)
-        second_product(0)
-        second_product(1)
-        weight_1(3)
-        weight_2(3)
-        filter_a(0)
-        filter_a(1)
+        correlate(0)
+        for q in range(1, CHUNKS):
+            correlate(q)
+            weight_factors(q - 1)
+            if q == LAST:
+                quantise_w2_w3()
+            weight(q - 1)
+        weight_factors(LAST)
+        weight(LAST)
+        for h in range(2):
+            for t in range(PACK):
+                second_product(h, t)
+        for q in range(CHUNKS):
+            apply_weight(q)
         make_hid(0)
-        make_hid(1)
-        finish(0)
-        filter_a(2)
-        finish(1)
-        filter_a(3)
-        make_hid(2)
-        make_hid(3)
-        finish(2)
-        make_hid(4)
-        finish(3)
-        finish(4)
+        for n in range(1, len(HID_PIECES)):
+            make_hid(n)
+            last_product(n - 1)
+        last_product(len(HID_PIECES) - 1)

from contextlib import ExitStack

import concourse.mybir as mybir
from concourse.masks import make_identity

K, T, S, D, N, H = 1024, 2048, 1024, 4, 128, 512
FLOPS = 2 * (2 * K * H * S + H * N * S)

F32 = mybir.dt.float32
BF16 = mybir.dt.bfloat16
I32 = mybir.dt.int32
U32 = mybir.dt.uint32
U16 = mybir.dt.uint16
U8 = mybir.dt.uint8
FP8X4 = mybir.dt.float8_e4m3fn_x4
ACT = mybir.ActivationFunctionType
MULT = mybir.AluOpType.mult
ADD = mybir.AluOpType.add
MAX = mybir.AluOpType.max

P = 128
PACK = 4
K_PASS = P * PACK
PASSES = K // K_PASS
QUADRANT = 32
LIST_COL = 16
BANK = 512
HALF = S // 2
CHUNKS = 4
SUMS = 2 * HALF // D
LAST = CHUNKS - 1

W1_LAST_PIECES = ((0, 64), (64, 96), (96, 128))
W2_PIECE = 32
SCALAR_TILE = 3
HID_PIECES = ((0, 0, 256), (0, 256, 512), (1, 0, 256), (1, 256, 384), (1, 384, 512))
IM_BANKS = (1, 3, 5)


def tile_picked_ycryoem_filt_p_kernel(
    tc, x_words, x_scales, w1, w2, ctf, unit, w3, offs, half, out
):
    nc = tc.nc
    with ExitStack() as ctx:
        keep = ctx.enter_context(tc.tile_pool(name="keep", bufs=1))
        ring = ctx.enter_context(tc.tile_pool(name="ring", bufs=2))
        psum = ctx.enter_context(tc.psum_pool(name="psum", bufs=1))

        def bank(b, name):
            return psum.tile([P, BANK], F32, name=name, tag="bank%d" % b)

        def pass_rows(w, g):
            return w[g * K_PASS : (g + 1) * K_PASS, :].rearrange("(p j) c -> p j c", j=PACK)

        def cols(h):
            return slice(h * HALF, (h + 1) * HALF)

        def entries(lst, h):
            return lst[:, h * HALF // LIST_COL : (h + 1) * HALF // LIST_COL]

        offs_sb = keep.tile([P, S // LIST_COL], U16, name="offs_sb")
        half_sb = keep.tile([P, S // LIST_COL], U16, name="half_sb")
        scale_table = keep.tile([P, T], U8, name="scale_table", align_bytes=64)
        nc.vector.memset(scale_table[:].bitcast(I32), 0)
        nc.sync.dma_start(offs_sb[:], offs)
        scale_rows = keep.tile([P, T // 4], I32, name="scale_rows")
        for r in range(P // QUADRANT):
            live = slice(QUADRANT * r, QUADRANT * r + 4 * PASSES)
            nc.sync.dma_start(scale_rows[live, :], x_scales[:, 4 * r : 4 * r + 4, :].bitcast(I32))
            nc.vector.tensor_copy(scale_table[live, :].bitcast(I32), scale_rows[live, :])

        w1_first = keep.tile([P, PACK, H], F32, name="w1_first", tag="first_pass")
        nc.sync.dma_start(w1_first[:], pass_rows(w1, 0))
        word_table = [keep.tile([P, T], I32, name="word_table%d" % g, align_bytes=64) for g in range(PASSES)]
        w1_last = [keep.tile([P, PACK, PACK * (m1 - m0)], F32, name="w1_last%d" % m0) for m0, m1 in W1_LAST_PIECES]

        def load_words(g):
            nc.sync.dma_start(word_table[g][:], x_words[g].rearrange("p n t -> p (n t)").bitcast(I32))

        def load_w1_last(n):
            m0, m1 = W1_LAST_PIECES[n]
            nc.sync.dma_start(w1_last[n][:], pass_rows(w1, 1)[:, :, PACK * m0 : PACK * m1])

        load_words(0)
        load_w1_last(0)
        load_words(1)
        load_w1_last(1)
        load_w1_last(2)
        nc.sync.dma_start(half_sb[:], half)
        ctf_sb = keep.tile([P, PACK, S], F32, name="ctf_sb")
        ident = keep.tile([P, P], F32, name="ident")
        make_identity(nc, ident[:])
        table_warm = keep.tile([P, 1], F32, name="table_warm")
        nc.scalar.activation(table_warm[:], ident[:, 0:1], ACT.Abs_reciprocal_sqrt, bias=1.0)

        def new_dealt():
            return ring.tile([P, PACK, P, PACK], BF16, name="dealt", tag="dealt", align_bytes=64)

        def deal(copy, dealt, raw, m0, m1):
            copy(
                dealt[:, :, m0:m1, :].rearrange("p t m j -> p m j t"),
                raw.rearrange("p j (m t) -> p m j t", t=PACK),
            )

        def weight_planes(name):
            codes = keep.tile([P, H], U32, name=name + "_codes", align_bytes=64)
            scales = keep.tile([P, H], U8, name=name + "_scales", align_bytes=64)
            return codes, scales

        def quantise(planes, dealt, t0, t1):
            nc.vector.quantize_mx(
                out=planes[0][:, t0 * P : t1 * P].bitcast(FP8X4),
                scales=planes[1][:, t0 * P : t1 * P],
                in_=dealt[:, t0:t1].rearrange("p t m j -> p (t m j)"),
            )

        x_scale = keep.tile([P, S], U8, name="x_scale", align_bytes=64)
        nc.vector.tensor_copy(x_scale[:], scale_table[:].indirect(offs_sb[:]))
        w1_planes = [weight_planes("w1_pass%d" % g) for g in range(PASSES)]
        dealt = new_dealt()
        for m0 in (0, P // 2):
            deal(nc.scalar.copy, dealt, w1_first[:, :, PACK * m0 : PACK * (m0 + P // 2)], m0, m0 + P // 2)
        quantise(w1_planes[0], dealt, 0, PACK)

        w2_raw = [
            keep.tile([P, PACK, H], F32, name="w2_first", tag="first_pass"),
            keep.tile([P, PACK, H], F32, name="w2_last"),
        ]
        for t in range(PACK):
            nc.sync.dma_start(ctf_sb[:, t, :], ctf.rearrange("(p t) j -> p t j", t=PACK)[:, t, :])
        for g in range(PASSES):
            nc.sync.dma_start(w2_raw[g][:], pass_rows(w2, g))
        unit_sb = keep.tile([P, PACK], F32, name="unit_sb")
        nc.sync.dma_start(unit_sb[:], unit.rearrange("(p t) o -> p (t o)", t=PACK))
        w3_raw = keep.tile([P, PACK, N], F32, name="w3_raw")
        nc.sync.dma_start(w3_raw[:], pass_rows(w3, 0))

        x_code = {}
        for g in range(PASSES):
            for h in range(2):
                x_code[g, h] = keep.tile([P, HALF], U32, name="x_code%d%d" % (g, h), align_bytes=64)
                nc.vector.tensor_copy(x_code[g, h][:], word_table[g][:].bitcast(U32).indirect(entries(offs_sb, h)))

        def mx_pass(acc, planes, g, t, h):
            nc.tensor.matmul_mx(
                out=acc[:],
                lhsT=planes[g][0][:, t * P : (t + 1) * P].bitcast(FP8X4),
                lhsT_scale=planes[g][1][:, t * P : (t + 1) * P],
                rhs=x_code[g, h][:].bitcast(FP8X4),
                rhs_scale=x_scale[4 * g : P, cols(h)],
                start=(g == 0),
                stop=(g == PASSES - 1),
            )

        re_ps = {}
        for h in range(2):
            for t in range(PACK):
                re_ps[t, h] = bank(PACK * h + t, "re_ps")
                mx_pass(re_ps[t, h], w1_planes, 0, t, h)

        dealt = new_dealt()
        for raw, (m0, m1) in zip(w1_last, W1_LAST_PIECES):
            deal(nc.scalar.copy, dealt, raw[:], m0, m1)
        for t in range(PACK):
            quantise(w1_planes[1], dealt, t, t + 1)

        re = [keep.tile([P, S], F32, name="re%d" % t) for t in range(PACK)]
        for t in range(PACK):
            for h in range(2):
                mx_pass(re_ps[t, h], w1_planes, 1, t, h)
                nc.scalar.copy(re[t][:, cols(h)], re_ps[t, h][:])

        ra = [keep.tile([P, PACK, HALF], F32, name="ra%d" % h) for h in range(2)]
        im_term = [keep.tile([P, PACK, HALF], F32, name="im_term%d" % h) for h in range(2)]
        ra_term = [keep.tile([P, PACK, HALF], F32, name="ra_term%d" % h) for h in range(2)]
        squares_ps, cross_ps, wien_ps, factors, hid = {}, {}, {}, {}, {}

        def chunk_tiles(q):
            return (2 * (q % 2), 2 * (q % 2) + 1)

        def new_members(name):
            return ring.tile([P, 2, SUMS, 2], F32, name=name, tag=name)

        def as_written(members):
            return members[:].rearrange("p a w b -> p w a b")

        def by_member(x):
            return x.rearrange("p t (v a b) -> p (t v) a b", a=2, b=2)

        def shell_sum(dst, members):
            for u in range(2):
                for d in range(D):
                    nc.tensor.matmul(
                        dst[:, u * P : (u + 1) * P],
                        members[:, d // 2, u * P : (u + 1) * P, d % 2],
                        ident[:],
                        start=(d == 0),
                        stop=(d == D - 1),
                        is_transpose=True,
                    )

        def correlate(q):
            h = q // 2
            rb = ring.tile([P, 2, HALF], F32, name="rb", tag="rb")
            for t in chunk_tiles(q):
                nc.vector.tensor_tensor(ra[h][:, t, :], re_ps[t, h][:], ctf_sb[:, t, cols(h)], MULT)
                partner = re[t][:].indirect(entries(half_sb, h))
                if t == SCALAR_TILE:
                    ah = ring.tile([P, HALF], F32, name="ah", tag="ah")
                    nc.scalar.activation(ah[:], partner, ACT.Copy)
                    partner = ah[:]
                nc.vector.tensor_tensor(rb[:, t % 2, :], partner, ctf_sb[:, t, cols(h)], MULT)
            t0, t1 = chunk_tiles(q)
            ra_q = ra[h][:, t0 : t1 + 1, :]
            pa = new_members("pa")
            nc.scalar.activation(as_written(pa), by_member(ra_q), ACT.Square)
            squares_ps[q] = bank(2 * q, "squares_ps")
            shell_sum(squares_ps[q][:, 0:SUMS], pa)
            pb = new_members("pb")
            nc.scalar.activation(as_written(pb), by_member(rb[:]), ACT.Square)
            shell_sum(squares_ps[q][:, SUMS : 2 * SUMS], pb)
            xc = new_members("xc")
            nc.vector.tensor_tensor(as_written(xc), by_member(ra_q), by_member(rb[:]), MULT)
            cross_ps[q] = bank(2 * q + 1, "cross_ps")
            shell_sum(cross_ps[q][:, 0:SUMS], xc)

        def small(name):
            return ring.tile([P, SUMS], F32, name=name, tag=name)

        def weight_factors(q):
            inv = ring.tile([P, 2 * SUMS], F32, name="inv", tag="inv")
            nc.scalar.activation(inv[:], squares_ps[q][:], ACT.Abs_reciprocal_sqrt, bias=0.3)
            part = small("part")
            nc.vector.tensor_tensor(part[:], cross_ps[q][:, 0:SUMS], inv[:, 0:SUMS], MULT)
            fsc = small("fsc")
            nc.vector.tensor_tensor(fsc[:], part[:], inv[:, SUMS : 2 * SUMS], MULT)
            mag = small("mag")
            nc.scalar.activation(mag[:], fsc[:], ACT.Abs)
            root = small("root")
            nc.scalar.activation(root[:], mag[:], ACT.Abs_reciprocal_sqrt, bias=0.5)
            factors[q] = (fsc, root)
            if q == LAST:
                recip = small("recip")
                top = small("top")
                nc.scalar.activation(top[:], fsc[:], ACT.Relu, bias=0.6)
                nc.scalar.activation(recip[:], root[:], ACT.Square)
                factors[q] = (top, recip)

        def weight(q):
            wien = small("wien")
            if q == LAST:
                top, recip = factors[q]
                nc.vector.tensor_tensor(wien[:], top[:], recip[:], MULT)
            else:
                fsc, root = factors[q]
                top = small("top")
                nc.vector.scalar_tensor_tensor(top[:], fsc[:], 0.6, root[:], ADD, MULT)
                nc.vector.scalar_tensor_tensor(wien[:], top[:], 0.0, root[:], MAX, MULT)
            wien_ps[q] = bank(2 * q, "wien_ps")
            for u in range(2):
                nc.tensor.transpose(wien_ps[q][:, u * P : (u + 1) * P], wien[:, u * P : (u + 1) * P], ident[:])

        w2_planes = [weight_planes("w2_pass%d" % g) for g in range(PASSES)]
        im_scale = keep.tile([P, PACK], F32, name="im_scale")
        w3_codes = keep.tile([P, N], U32, name="w3_codes", align_bytes=64)
        w3_scales = keep.tile([P, N], U8, name="w3_scales", align_bytes=64)

        def quantise_w2_w3():
            for g, copy in enumerate((nc.vector.tensor_copy, nc.scalar.copy)):
                w2_dealt = new_dealt()
                for m0 in range(0, P, W2_PIECE):
                    m1 = m0 + W2_PIECE
                    deal(copy, w2_dealt, w2_raw[g][:, :, PACK * m0 : PACK * m1], m0, m1)
                quantise(w2_planes[g], w2_dealt, 0, PACK)
            nc.vector.tensor_scalar(im_scale[:], unit_sb[:], -0.4, None, MULT)
            w3_words = keep.tile([P, N, PACK], BF16, name="w3_words", align_bytes=64)
            nc.scalar.copy(w3_words[:], w3_raw[:].rearrange("p j m -> p m j"))
            nc.vector.quantize_mx(
                out=w3_codes[:].bitcast(FP8X4), scales=w3_scales[:], in_=w3_words[:].rearrange("p m j -> p (m j)")
            )

        def second_product(h, t):
            acc = bank(IM_BANKS[(PACK * h + t) % len(IM_BANKS)], "im_ps")
            for g in range(PASSES):
                mx_pass(acc, w2_planes, g, t, h)
            nc.scalar.activation(im_term[h][:, t, :], acc[:], ACT.Copy, scale=im_scale[:, t : t + 1])

        def apply_weight(q):
            h = q // 2
            for t in chunk_tiles(q):
                nc.vector.scalar_tensor_tensor(
                    ra_term[h][:, t, :].rearrange("p (v d) -> p v d", d=D),
                    wien_ps[q][:, (t % 2) * P : (t % 2 + 1) * P].unsqueeze(2).to_broadcast([P, P, D]),
                    unit_sb[:, t : t + 1],
                    ra[h][:, t, :].rearrange("p (v d) -> p v d", d=D),
                    MULT,
                    MULT,
                )

        def make_hid(n):
            h, c0, c1 = HID_PIECES[n]
            hid[n] = ring.tile([P, c1 - c0, PACK], BF16, name="hid", tag="hid", align_bytes=64)
            nc.vector.tensor_tensor(
                hid[n][:].rearrange("p (c i) t -> p c t i", i=4),
                ra_term[h][:, :, c0:c1].rearrange("p t (c i) -> p c t i", i=4),
                im_term[h][:, :, c0:c1].rearrange("p t (c i) -> p c t i", i=4),
                ADD,
            )

        def last_product(n):
            h, c0, c1 = HID_PIECES[n]
            width = c1 - c0
            codes = ring.tile([P, width], U32, name="hid_codes", tag="hid_codes", align_bytes=64)
            scales = ring.tile([P, width], U8, name="hid_scales", tag="hid_scales", align_bytes=64)
            nc.vector.quantize_mx(
                out=codes[:].bitcast(FP8X4), scales=scales[:], in_=hid[n][:].rearrange("p c t -> p (c t)")
            )
            acc = bank(2 * (n % CHUNKS), "out_ps")
            nc.tensor.matmul_mx(
                out=acc[:, 0:width],
                lhsT=w3_codes[:].bitcast(FP8X4),
                lhsT_scale=w3_scales[:],
                rhs=codes[:].bitcast(FP8X4),
                rhs_scale=scales[:],
                start=True,
                stop=True,
            )
            res = ring.tile([P, width], F32, name="res", tag="res", bufs=3)
            nc.scalar.copy(res[:], acc[:, 0:width])
            nc.sync.dma_start(out[:, h * HALF + c0 : h * HALF + c1], res[:])

        correlate(0)
        for q in range(1, CHUNKS):
            correlate(q)
            weight_factors(q - 1)
            if q == LAST:
                quantise_w2_w3()
            weight(q - 1)
        weight_factors(LAST)
        weight(LAST)
        for h in range(2):
            for t in range(PACK):
                second_product(h, t)
        for q in range(CHUNKS):
            apply_weight(q)
        make_hid(0)
        for n in range(1, len(HID_PIECES)):
            make_hid(n)
            last_product(n - 1)
        last_product(len(HID_PIECES) - 1)
